import numpy as np
import ml_dtypes


def mxq(x, axis, fmt="e4m3"):
    dtype, down = {"e4m3": (ml_dtypes.float8_e4m3fn, 7), "e5m2": (ml_dtypes.float8_e5m2, 14)}[fmt]
    v = np.moveaxis(np.asarray(x, np.float32).astype(ml_dtypes.bfloat16).astype(np.float64), axis, -1)
    blocks = v.reshape(v.shape[:-1] + (-1, 32))
    amax = np.abs(blocks).max(-1, keepdims=True)
    byte = np.maximum(np.where(amax > 0, np.frexp(amax)[1] - 1 + 127, 0) - down, 1)
    scale = np.exp2(byte - 127.0)
    codes = (blocks / scale).astype(np.float32).astype(dtype).astype(np.float64)
    return np.moveaxis((codes * scale).reshape(v.shape), -1, axis)


WIDE = False


def mx_kscale(k):
    if not WIDE:
        return np.ones(k)
    levels = np.array([10, -10, 5, -5, 0])
    if k % 512:
        return np.exp2(np.random.permutation(np.resize(levels, k // 32))).repeat(32)
    a = np.empty((k // 512, 16))
    for p in range(k // 512):
        a[p, :8] = np.random.permutation(np.resize(levels, 8))
        for g in range(8):
            far = levels[np.abs(levels - a[p, g]) >= 10]
            a[p, g + 8] = far[np.random.randint(len(far))]
    return np.exp2(a.ravel()).repeat(32)


def f64(x):
    return np.asarray(x).astype(np.float64)


def striped(idx):
    return np.tile(idx.reshape(-1, 16).T, (8, 1)).astype(np.uint16)


def unstriped(offs):
    return offs[:16].T.reshape(-1).astype(np.int64)


def striped8(idx):
    return np.concatenate([x.reshape(-1, 16).T for x in idx]).astype(np.uint16)


def runs(offs, k):
    lists = np.stack([offs[16 * r : 16 * r + 16].T.reshape(-1) for r in range(8)]).astype(np.int64)
    return lists[np.arange(k) % 512 // 64]


def pack_weight(w):
    k, n = w.shape
    w = f64(np.asarray(w, np.float32).astype(ml_dtypes.bfloat16)).reshape(k // 32, 32, n)
    amax = np.abs(w).max(1)
    byte = np.clip(np.where(amax > 0, np.frexp(amax)[1] - 1 + 127 - 7, 1), 1, 254)
    scaled = (w * np.exp2(127.0 - byte)[:, None, :]).reshape(k, n).astype(np.float32)
    words = np.ascontiguousarray(scaled.reshape(k // 512, 128, 4, n).transpose(0, 1, 3, 2)).astype(ml_dtypes.float8_e4m3fn).view(np.uint8)
    return words, np.ascontiguousarray(byte.astype(np.uint8).reshape(k // 512, 16, n))


def unpack_weight(words, scales):
    g, p, n, _ = words.shape
    vals = np.ascontiguousarray(words).view(ml_dtypes.float8_e4m3fn).astype(np.float64) * np.repeat(np.exp2(scales.astype(np.float64) - 127.0), 8, axis=1)[..., None]
    return vals.transpose(0, 1, 3, 2).reshape(g * 512, n)


def sigmoid(v):
    return 1.0 / (1.0 + np.exp(-np.maximum(v, -700.0)))

def planes(y):
    n, m = y.shape
    v = y.astype(np.float32).astype(ml_dtypes.bfloat16).astype(np.float64).reshape(n // 32, 32, m)
    top = np.abs(v).max(1)
    byte = np.clip(np.where(top > 0, np.frexp(top)[1] - 1 + 127 - 7, 1), 1, 254)
    codes = (v * np.exp2(127.0 - byte)[:, None, :]).reshape(n, m).astype(np.float32).astype(ml_dtypes.float8_e4m3fn).view(np.uint8)
    words = codes.reshape(n // 512, 128, 4, m).transpose(0, 1, 3, 2)
    return np.ascontiguousarray(words), np.ascontiguousarray(byte.astype(np.uint8).reshape(n // 512, 16, m))


K, T, S, N, H, J = 512, 2048, 256, 512, 512, 512


def setup_inputs():
    n = np.random.standard_normal
    s = mx_kscale(K)[:, None]
    u = mx_kscale(H)
    packed_xT = pack_weight(n((K, T)) * s)
    packed_w1 = pack_weight(n((K, H)) / np.sqrt(K) / s)
    packed_w2 = pack_weight(n((H, N)) / np.sqrt(H) / u[:, None])
    return {
        "x_words": packed_xT[0],
        "x_scales": packed_xT[1],
        "w1_words": packed_w1[0],
        "w1_scales": packed_w1[1],
        "gn": (np.random.uniform(0.5, 1.5, (H, 1)) * u[:, None]).astype(np.float32),
        "w2_words": packed_w2[0],
        "w2_scales": packed_w2[1],
        "offs": striped(np.random.permutation(T)[:S]),
        "n1": striped(np.random.randint(0, S, J)),
        "n2": striped8(np.stack([np.random.permutation(S) for _ in range(8)])),
        "n3": striped8(np.stack([np.random.permutation(S) for _ in range(8)])),
        "n4": striped8(np.stack([np.random.permutation(S) for _ in range(8)])),
    }


def reference(x_words, x_scales, w1_words, w1_scales, gn, w2_words, w2_scales, offs, n1, n2, n3, n4):
    xq = unpack_weight(x_words, x_scales)[:, unstriped(offs)]
    y = unpack_weight(w1_words, w1_scales).T @ xq
    mb = y[:, unstriped(n1)]
    mn = mb.reshape(H, S, 2).min(axis=2)
    mx = mb.reshape(H, S, 2).max(axis=2)
    z = f64(gn) * ((y - mn) * sigmoid(mx))
    h = unpack_weight(w2_words, w2_scales).T @ mxq(z, 0, "e4m3")
    out_0 = np.maximum(h, h[np.arange(N)[:, None], runs(n2, N)]) - (np.maximum(h[np.arange(N)[:, None], runs(n3, N)], h[np.arange(N)[:, None], runs(n4, N)]))
    return (out_0,) + planes(out_0)

@@ -1,0 +1,237 @@
+from contextlib import ExitStack
+
+import concourse.mybir as mybir
+
+K, T, S, N, H, J = 512, 2048, 256, 512, 512, 512
+FLOPS = 2 * K * H * S + 2 * H * N * S
+
+F32 = mybir.dt.float32
+BF16 = mybir.dt.bfloat16
+I32 = mybir.dt.int32
+U32 = mybir.dt.uint32
+U16 = mybir.dt.uint16
+U8 = mybir.dt.uint8
+FP8X4 = mybir.dt.float8_e4m3fn_x4
+ALU = mybir.AluOpType
+ACT = mybir.ActivationFunctionType
+
+P = 128
+PACK = 4
+HALF = S // 2
+Y_WINDOW = J + 16
+H_WINDOW = 2 * S
+
+
+def load_scale_rows(queue, tile, scales, q):
+    queue.dma_start(out=tile[32 * q : 32 * q + 4, :].bitcast(I32), in_=scales[0, 4 * q : 4 * q + 4, :].bitcast(I32))
+
+
+def words_of(packed):
+    return packed[0].rearrange("p n t -> p (n t)").bitcast(I32)
+
+
+def deal(nc, dealt, raw):
+    nc.vector.tensor_copy(out=dealt.rearrange("p (t m) -> p m t", t=PACK), in_=raw.rearrange("p (m t) -> p m t", t=PACK))
+
+
+def tile_picked_layghardmix_none_po_kernel(
+    tc, x_words, x_scales, w1_words, w1_scales, gn, w2_words, w2_scales, offs, n1, n2, n3, n4, out_0, out_1, out_2
+):
+    nc = tc.nc
+    with ExitStack() as ctx:
+        keep = ctx.enter_context(tc.tile_pool(name="keep", bufs=1))
+        ring = ctx.enter_context(tc.tile_pool(name="ring", bufs=2))
+        psum = ctx.enter_context(tc.psum_pool(name="psum", bufs=1))
+
+        offs_sb = keep.tile([P, S // 16], U16, name="offs_sb")
+        n1_sb = keep.tile([P, J // 16], U16, name="n1_sb")
+        n2_sb = keep.tile([P, S // 16], U16, name="n2_sb")
+        n3_sb = keep.tile([P, S // 16], U16, name="n3_sb")
+        n4_sb = keep.tile([P, S // 16], U16, name="n4_sb")
+
+        x_w = keep.tile([P, T], I32, name="x_w")
+        x_s = keep.tile([P, T], U8, name="x_s")
+        raw_w = keep.tile([P, H], I32, name="raw_w")
+        raw_s = keep.tile([P, H], U8, name="raw_s")
+        gain = keep.tile([P, PACK], F32, name="gain")
+
+        nc.vector.memset(x_s[:].bitcast(I32), 0)
+        nc.vector.memset(raw_s[:].bitcast(I32), 0)
+
+        nc.scalar.dma_start(out=raw_w[:], in_=words_of(w1_words))
+        nc.sync.dma_start(offs_sb[:], offs)
+        nc.sync.dma_start(n1_sb[:], n1)
+        nc.sync.dma_start(n3_sb[:], n3)
+        nc.sync.dma_start(n4_sb[:], n4)
+        nc.sync.dma_start(n2_sb[:], n2)
+        nc.sync.dma_start(out=x_w[:], in_=words_of(x_words))
+        for q in range(4):
+            load_scale_rows(nc.scalar, x_s, x_scales, q)
+        for q in range(4):
+            load_scale_rows(nc.sync if q < 3 else nc.gpsimd, raw_s, w1_scales, q)
+        nc.gpsimd.dma_start(out=gain[:], in_=gn.rearrange("(p t) o -> p (t o)", t=PACK))
+
+        y_win = [keep.tile([P, Y_WINDOW], F32, name=f"y_win{t}") for t in range(PACK)]
+        h_win = [keep.tile([P, H_WINDOW], F32, name=f"h_win{t}") for t in range(PACK)]
+        for t in range(PACK):
+            nc.vector.memset(y_win[t][:, S:], 0.0)
+        for t in range(PACK):
+            nc.vector.memset(h_win[t][:, S:], 0.0)
+
+        w1_wd = keep.tile([P, H], U32, name="w1_wd", align_bytes=64)
+        w1_sd = keep.tile([P, H], U8, name="w1_sd", align_bytes=64)
+        w2_wd = keep.tile([P, N], U32, name="w2_wd", align_bytes=64)
+        w2_sd = keep.tile([P, N], U8, name="w2_sd", align_bytes=64)
+        xg_w = keep.tile([P, S], U32, name="xg_w", align_bytes=64)
+        xg_s = keep.tile([P, S], U8, name="xg_s", align_bytes=64)
+
+        deal(nc, w1_wd[:], raw_w[:].bitcast(U32))
+        nc.vector.tensor_copy(out=xg_s[:], in_=x_s[:].indirect(offs_sb[:]))
+        deal(nc, w1_sd[:], raw_s[:])
+        nc.sync.dma_start(out=raw_w[:], in_=words_of(w2_words))
+        for q in range(4):
+            load_scale_rows(nc.sync, raw_s, w2_scales, q)
+        nc.vector.tensor_copy(out=xg_w[:], in_=x_w[:].bitcast(U32).indirect(offs_sb[:]))
+
+        y_ps = [psum.tile([P, S], F32, name=f"y_ps{t}") for t in range(PACK)]
+        h_ps = [psum.tile([P, S], F32, name=f"h_ps{t}") for t in range(PACK)]
+        for t in range(PACK):
+            cols = slice(t * P, (t + 1) * P)
+            nc.tensor.matmul_mx(
+                out=y_ps[t][:],
+                lhsT=w1_wd[:, cols].bitcast(FP8X4),
+                lhsT_scale=w1_sd[:, cols],
+                rhs=xg_w[:].bitcast(FP8X4),
+                rhs_scale=xg_s[:],
+                start=True,
+                stop=True,
+            )
+        nc.scalar.copy(out=y_win[0][:, :S], in_=y_ps[0][:])
+        for t in range(1, PACK):
+            nc.vector.tensor_copy(out=y_win[t][:, :S], in_=y_ps[t][:])
+
+        z_planes = keep.tile([P, 2, PACK, HALF], BF16, name="z_planes")
+        lows = keep.tile([P, PACK, S], F32, name="lows")
+        highs = keep.tile([P, PACK, S], F32, name="highs")
+        gates = keep.tile([P, PACK, S], F32, name="gates")
+        spans = keep.tile([P, PACK, S], F32, name="spans")
+        pieces = [(0, 0, S), (1, 0, S), (2, 0, S), (3, 0, HALF), (3, HALF, S)]
+        members = {}
+
+        def fetch(piece):
+            t, j0, j1 = piece
+            if t not in members:
+                members[t] = ring.tile([P, J], F32, name="members")
+            nc.scalar.activation(members[t][:, 2 * j0 : 2 * j1], y_win[t][:].indirect(n1_sb[:, j0 // 8 : j1 // 8]), ACT.Copy)
+
+        def pair(piece):
+            t, j0, j1 = piece
+            both = members[t][:, 2 * j0 : 2 * j1].rearrange("p (j e) -> p j e", e=2)
+            return both[:, :, 0], both[:, :, 1]
+
+        def high(piece):
+            t, j0, j1 = piece
+            a, b = pair(piece)
+            nc.vector.tensor_tensor(highs[:, t, j0:j1], a, b, ALU.max)
+
+        def low(piece):
+            t, j0, j1 = piece
+            a, b = pair(piece)
+            nc.vector.tensor_tensor(lows[:, t, j0:j1], a, b, ALU.min)
+
+        def gate(piece):
+            t, j0, j1 = piece
+            nc.scalar.activation(gates[:, t, j0:j1], highs[:, t, j0:j1], ACT.Sigmoid)
+
+        def span(piece):
+            t, j0, j1 = piece
+            nc.vector.tensor_tensor(spans[:, t, j0:j1], y_win[t][:, j0:j1], lows[:, t, j0:j1], ALU.subtract)
+
+        def mix(piece):
+            t, j0, j1 = piece
+            nc.vector.scalar_tensor_tensor(
+                z_planes[:, j0 // HALF : j1 // HALF, t, :],
+                spans[:, t, j0:j1].rearrange("p (u j) -> p u j", j=HALF),
+                gain[:, t : t + 1],
+                gates[:, t, j0:j1].rearrange("p (u j) -> p u j", j=HALF),
+                ALU.mult,
+                ALU.mult,
+            )
+
+        fetch(pieces[0])
+        for i, piece in enumerate(pieces):
+            if i + 1 < len(pieces):
+                fetch(pieces[i + 1])
+            high(piece)
+            gate(piece)
+            low(piece)
+            if i > 0:
+                mix(pieces[i - 1])
+            span(piece)
+            if i == 0:
+                deal(nc, w2_wd[:], raw_w[:].bitcast(U32))
+                deal(nc, w2_sd[:], raw_s[:])
+        mix(pieces[-1])
+
+        z_w = keep.tile([P, S], U32, name="z_w", align_bytes=64)
+        z_s = keep.tile([P, S], U8, name="z_s", align_bytes=64)
+        z_rows = [keep.tile([P, HALF, PACK], BF16, name=f"z_rows{u}", align_bytes=64) for u in range(2)]
+        nc.scalar.copy(out=z_rows[0][:], in_=z_planes[:, 0].rearrange("p t j -> p j t"))
+        nc.vector.tensor_copy(out=z_rows[1][:], in_=z_planes[:, 1].rearrange("p t j -> p j t"))
+        for u in range(2):
+            half = slice(u * HALF, (u + 1) * HALF)
+            nc.vector.quantize_mx(
+                out=z_w[:, half].bitcast(FP8X4), scales=z_s[:, half], in_=z_rows[u][:].rearrange("p j t -> p (j t)")
+            )
+            for t in range(PACK):
+                cols = slice(t * P, (t + 1) * P)
+                nc.tensor.matmul_mx(
+                    out=h_ps[t][:, half],
+                    lhsT=w2_wd[:, cols].bitcast(FP8X4),
+                    lhsT_scale=w2_sd[:, cols],
+                    rhs=z_w[:, half].bitcast(FP8X4),
+                    rhs_scale=z_s[:, half],
+                    start=True,
+                    stop=True,
+                )
+            nc.scalar.copy(out=h_win[0][:, half], in_=h_ps[0][:, half])
+        for t in range(1, PACK):
+            nc.vector.tensor_copy(out=h_win[t][:, :S], in_=h_ps[t][:])
+
+        result = keep.tile([P, 2, PACK, HALF], F32, name="result")
+        o_rows = [keep.tile([P, HALF, PACK], BF16, name=f"o_rows{u}", align_bytes=64) for u in range(2)]
+        o_w = keep.tile([P, S], I32, name="o_w", align_bytes=64)
+        o_s = keep.tile([P, S], U8, name="o_s", align_bytes=64)
+        out_rows = out_0.rearrange("(p t) (u j) -> p u t j", t=PACK, j=HALF)
+        out_words = words_of(out_1)
+        for t, j0, j1 in pieces:
+            width = j1 - j0
+            at3 = ring.tile([P, width], F32, name="at3")
+            at4 = ring.tile([P, width], F32, name="at4")
+            at2 = ring.tile([P, width], F32, name="at2")
+            right = ring.tile([P, width], F32, name="right")
+            left = ring.tile([P, width], F32, name="left")
+            entries = slice(j0 // 16, j1 // 16)
+            nc.scalar.activation(at3[:], h_win[t][:].indirect(n3_sb[:, entries]), ACT.Copy)
+            nc.scalar.activation(at4[:], h_win[t][:].indirect(n4_sb[:, entries]), ACT.Copy)
+            nc.scalar.activation(at2[:], h_win[t][:].indirect(n2_sb[:, entries]), ACT.Copy)
+            nc.vector.tensor_tensor(right[:], at3[:], at4[:], ALU.max)
+            nc.vector.tensor_tensor(left[:], h_win[t][:, j0:j1], at2[:], ALU.max)
+            halves = slice(j0 // HALF, j1 // HALF)
+            nc.vector.tensor_tensor(
+                result[:, halves, t, :],
+                left[:].rearrange("p (u j) -> p u j", j=HALF),
+                right[:].rearrange("p (u j) -> p u j", j=HALF),
+                ALU.subtract,
+            )
+            nc.sync.dma_start(out=out_rows[:, halves, t, :], in_=result[:, halves, t, :])
+            if t == PACK - 1:
+                u = j0 // HALF
+                nc.vector.tensor_copy(out=o_rows[u][:], in_=result[:, u].rearrange("p t j -> p j t"))
+                nc.vector.quantize_mx(
+                    out=o_w[:, j0:j1].bitcast(FP8X4), scales=o_s[:, j0:j1], in_=o_rows[u][:].rearrange("p j t -> p (j t)")
+                )
+                nc.sync.dma_start(out=out_words[:, j0:j1], in_=o_w[:, j0:j1])
+        for q in range(4):
+            queue = nc.scalar if q < 3 else nc.sync
+            queue.dma_start(out=out_2[0, 4 * q : 4 * q + 4, :].bitcast(I32), in_=o_s[32 * q : 32 * q + 4, :].bitcast(I32))

@@ -26,11 +26,23 @@ def load_scale_rows(queue, tile, scales, q):
     queue.dma_start(out=tile[32 * q : 32 * q + 4, :].bitcast(I32), in_=scales[0, 4 * q : 4 * q + 4, :].bitcast(I32))
 
 
+def load_scale_rows_spread(queue, tile, scales, q):
+    queue.dma_start(
+        out=tile[32 * q : 32 * q + 32, :].bitcast(I32), in_=scales[0, 4 * q : 4 * q + 4, :].bitcast(I32).partition_broadcast(8)
+    )
+
+
 def words_of(packed):
     return packed[0].rearrange("p n t -> p (n t)").bitcast(I32)
 
 
-def deal(nc, dealt, raw):
+def deal_scales(nc, dealt, raw, t0, t1):
+    nc.vector.tensor_copy(
+        out=dealt.rearrange("p (t m) -> p t m", t=PACK)[:, t0:t1, :], in_=raw.rearrange("p (m t) -> p t m", t=PACK)[:, t0:t1, :]
+    )
+
+
+def deal_words(nc, dealt, raw):
     nc.vector.tensor_copy(out=dealt.rearrange("p (t m) -> p m t", t=PACK), in_=raw.rearrange("p (m t) -> p m t", t=PACK))
 
 
@@ -49,27 +61,32 @@ def tile_picked_layghardmix_none_po_kernel(
         n3_sb = keep.tile([P, S // 16], U16, name="n3_sb")
         n4_sb = keep.tile([P, S // 16], U16, name="n4_sb")
 
-        x_w = keep.tile([P, T], I32, name="x_w")
-        x_s = keep.tile([P, T], U8, name="x_s")
-        raw_w = keep.tile([P, H], I32, name="raw_w")
-        raw_s = keep.tile([P, H], U8, name="raw_s")
+        x_w = keep.tile([P, T], I32, name="x_w", tag="x words, dealt w1 scales", align_bytes=64)
+        x_s = keep.tile([P, T], U8, name="x_s", tag="x scales, picked words", align_bytes=64)
+        w1_w = keep.tile([P, H], I32, name="w1_w")
+        w1_s = keep.tile([P, H], U8, name="w1_s", tag="w1 scales, dealt w2 words", align_bytes=64)
+        w2_w = keep.tile([P, N], I32, name="w2_w", tag="w2 words, dealt w2 scales", align_bytes=64)
+        w2_s = keep.tile([P, N], U8, name="w2_s")
         gain = keep.tile([P, PACK], F32, name="gain")
 
         nc.vector.memset(x_s[:].bitcast(I32), 0)
-        nc.vector.memset(raw_s[:].bitcast(I32), 0)
 
-        nc.scalar.dma_start(out=raw_w[:], in_=words_of(w1_words))
         nc.sync.dma_start(offs_sb[:], offs)
+        nc.sync.dma_start(out=w1_w[:], in_=words_of(w1_words))
+        load_scale_rows_spread(nc.scalar, w1_s, w1_scales, 0)
+        for q in range(4):
+            load_scale_rows(nc.sync if q < 2 else nc.scalar, x_s, x_scales, q)
+        nc.sync.dma_start(out=x_w[:], in_=words_of(x_words))
+        for q in range(1, 4):
+            load_scale_rows_spread(nc.sync, w1_s, w1_scales, q)
         nc.sync.dma_start(n1_sb[:], n1)
+        nc.sync.dma_start(out=w2_w[:], in_=words_of(w2_words))
+        for q in range(4):
+            load_scale_rows_spread(nc.sync, w2_s, w2_scales, q)
+        nc.sync.dma_start(out=gain[:], in_=gn.rearrange("(p t) o -> p (t o)", t=PACK))
         nc.sync.dma_start(n3_sb[:], n3)
         nc.sync.dma_start(n4_sb[:], n4)
         nc.sync.dma_start(n2_sb[:], n2)
-        nc.sync.dma_start(out=x_w[:], in_=words_of(x_words))
-        for q in range(4):
-            load_scale_rows(nc.scalar, x_s, x_scales, q)
-        for q in range(4):
-            load_scale_rows(nc.sync if q < 3 else nc.gpsimd, raw_s, w1_scales, q)
-        nc.gpsimd.dma_start(out=gain[:], in_=gn.rearrange("(p t) o -> p (t o)", t=PACK))
 
         y_win = [keep.tile([P, Y_WINDOW], F32, name=f"y_win{t}") for t in range(PACK)]
         h_win = [keep.tile([P, H_WINDOW], F32, name=f"h_win{t}") for t in range(PACK)]
@@ -77,21 +94,18 @@ def tile_picked_layghardmix_none_po_kernel(
             nc.vector.memset(y_win[t][:, S:], 0.0)
         for t in range(PACK):
             nc.vector.memset(h_win[t][:, S:], 0.0)
+        warm = keep.tile([P, 1], F32, name="warm")
+        nc.scalar.activation(warm[:], y_win[0][:, S : S + 1], ACT.Sigmoid)
 
         w1_wd = keep.tile([P, H], U32, name="w1_wd", align_bytes=64)
-        w1_sd = keep.tile([P, H], U8, name="w1_sd", align_bytes=64)
-        w2_wd = keep.tile([P, N], U32, name="w2_wd", align_bytes=64)
-        w2_sd = keep.tile([P, N], U8, name="w2_sd", align_bytes=64)
-        xg_w = keep.tile([P, S], U32, name="xg_w", align_bytes=64)
+        deal_words(nc, w1_wd[:], w1_w[:].bitcast(U32))
         xg_s = keep.tile([P, S], U8, name="xg_s", align_bytes=64)
-
-        deal(nc, w1_wd[:], raw_w[:].bitcast(U32))
         nc.vector.tensor_copy(out=xg_s[:], in_=x_s[:].indirect(offs_sb[:]))
-        deal(nc, w1_sd[:], raw_s[:])
-        nc.sync.dma_start(out=raw_w[:], in_=words_of(w2_words))
-        for q in range(4):
-            load_scale_rows(nc.sync, raw_s, w2_scales, q)
+        xg_w = keep.tile([P, S], U32, name="xg_w", tag="x scales, picked words", align_bytes=64)
         nc.vector.tensor_copy(out=xg_w[:], in_=x_w[:].bitcast(U32).indirect(offs_sb[:]))
+        w1_sd = keep.tile([P, H], U8, name="w1_sd", tag="x words, dealt w1 scales", align_bytes=64)
+        deal_scales(nc, w1_sd[:], w1_s[:], 0, 1)
+        deal_scales(nc, w1_sd[:], w1_s[:], 1, PACK)
 
         y_ps = [psum.tile([P, S], F32, name=f"y_ps{t}") for t in range(PACK)]
         h_ps = [psum.tile([P, S], F32, name=f"h_ps{t}") for t in range(PACK)]
@@ -117,16 +131,15 @@ def tile_picked_layghardmix_none_po_kernel(
         spans = keep.tile([P, PACK, S], F32, name="spans")
         pieces = [(0, 0, S), (1, 0, S), (2, 0, S), (3, 0, HALF), (3, HALF, S)]
         members = {}
+        z_rows = [keep.tile([P, HALF, PACK], BF16, name=f"z_rows{u}", align_bytes=64) for u in range(2)]
 
         def fetch(piece):
             t, j0, j1 = piece
-            if t not in members:
-                members[t] = ring.tile([P, J], F32, name="members")
-            nc.scalar.activation(members[t][:, 2 * j0 : 2 * j1], y_win[t][:].indirect(n1_sb[:, j0 // 8 : j1 // 8]), ACT.Copy)
+            members[piece] = ring.tile([P, 2 * (j1 - j0)], F32, name="members")
+            nc.scalar.activation(members[piece][:], y_win[t][:].indirect(n1_sb[:, j0 // 8 : j1 // 8]), ACT.Copy)
 
         def pair(piece):
-            t, j0, j1 = piece
-            both = members[t][:, 2 * j0 : 2 * j1].rearrange("p (j e) -> p j e", e=2)
+            both = members[piece][:].rearrange("p (j e) -> p j e", e=2)
             return both[:, :, 0], both[:, :, 1]
 
         def high(piece):
@@ -158,6 +171,8 @@ def tile_picked_layghardmix_none_po_kernel(
                 ALU.mult,
             )
 
+        w2_wd = keep.tile([P, N], U32, name="w2_wd", tag="w1 scales, dealt w2 words", align_bytes=64)
+        deal_words(nc, w2_wd[:], w2_w[:].bitcast(U32))
         fetch(pieces[0])
         for i, piece in enumerate(pieces):
             if i + 1 < len(pieces):
@@ -165,17 +180,16 @@ def tile_picked_layghardmix_none_po_kernel(
             high(piece)
             gate(piece)
             low(piece)
-            if i > 0:
+            if i == 0:
+                w2_sd = keep.tile([P, N], U8, name="w2_sd", tag="w2 words, dealt w2 scales", align_bytes=64)
+                deal_scales(nc, w2_sd[:], w2_s[:], 0, PACK)
+            else:
                 mix(pieces[i - 1])
             span(piece)
-            if i == 0:
-                deal(nc, w2_wd[:], raw_w[:].bitcast(U32))
-                deal(nc, w2_sd[:], raw_s[:])
         mix(pieces[-1])
 
         z_w = keep.tile([P, S], U32, name="z_w", align_bytes=64)
         z_s = keep.tile([P, S], U8, name="z_s", align_bytes=64)
-        z_rows = [keep.tile([P, HALF, PACK], BF16, name=f"z_rows{u}", align_bytes=64) for u in range(2)]
         nc.scalar.copy(out=z_rows[0][:], in_=z_planes[:, 0].rearrange("p t j -> p j t"))
         nc.vector.tensor_copy(out=z_rows[1][:], in_=z_planes[:, 1].rearrange("p t j -> p j t"))
         for u in range(2):
@@ -204,20 +218,20 @@ def tile_picked_layghardmix_none_po_kernel(
         o_s = keep.tile([P, S], U8, name="o_s", align_bytes=64)
         out_rows = out_0.rearrange("(p t) (u j) -> p u t j", t=PACK, j=HALF)
         out_words = words_of(out_1)
+
         for t, j0, j1 in pieces:
-            width = j1 - j0
-            at3 = ring.tile([P, width], F32, name="at3")
-            at4 = ring.tile([P, width], F32, name="at4")
-            at2 = ring.tile([P, width], F32, name="at2")
-            right = ring.tile([P, width], F32, name="right")
-            left = ring.tile([P, width], F32, name="left")
+            at3 = ring.tile([P, j1 - j0], F32, name="at3")
+            at4 = ring.tile([P, j1 - j0], F32, name="at4")
+            at2 = ring.tile([P, j1 - j0], F32, name="at2")
+            right = ring.tile([P, j1 - j0], F32, name="right")
+            left = ring.tile([P, j1 - j0], F32, name="left")
             entries = slice(j0 // 16, j1 // 16)
+            halves = slice(j0 // HALF, j1 // HALF)
             nc.scalar.activation(at3[:], h_win[t][:].indirect(n3_sb[:, entries]), ACT.Copy)
             nc.scalar.activation(at4[:], h_win[t][:].indirect(n4_sb[:, entries]), ACT.Copy)
             nc.scalar.activation(at2[:], h_win[t][:].indirect(n2_sb[:, entries]), ACT.Copy)
             nc.vector.tensor_tensor(right[:], at3[:], at4[:], ALU.max)
             nc.vector.tensor_tensor(left[:], h_win[t][:, j0:j1], at2[:], ALU.max)
-            halves = slice(j0 // HALF, j1 // HALF)
             nc.vector.tensor_tensor(
                 result[:, halves, t, :],
                 left[:].rearrange("p (u j) -> p u j", j=HALF),
@@ -225,13 +239,14 @@ def tile_picked_layghardmix_none_po_kernel(
                 ALU.subtract,
             )
             nc.sync.dma_start(out=out_rows[:, halves, t, :], in_=result[:, halves, t, :])
-            if t == PACK - 1:
-                u = j0 // HALF
-                nc.vector.tensor_copy(out=o_rows[u][:], in_=result[:, u].rearrange("p t j -> p j t"))
-                nc.vector.quantize_mx(
-                    out=o_w[:, j0:j1].bitcast(FP8X4), scales=o_s[:, j0:j1], in_=o_rows[u][:].rearrange("p j t -> p (j t)")
-                )
-                nc.sync.dma_start(out=out_words[:, j0:j1], in_=o_w[:, j0:j1])
+        nc.scalar.copy(out=o_rows[0][:], in_=result[:, 0].rearrange("p t j -> p j t"))
+        nc.vector.tensor_copy(out=o_rows[1][:], in_=result[:, 1].rearrange("p t j -> p j t"))
+        for u in range(2):
+            half = slice(u * HALF, (u + 1) * HALF)
+            nc.vector.quantize_mx(
+                out=o_w[:, half].bitcast(FP8X4), scales=o_s[:, half], in_=o_rows[u][:].rearrange("p j t -> p (j t)")
+            )
+            nc.sync.dma_start(out=out_words[:, half], in_=o_w[:, half])
         for q in range(4):
-            queue = nc.scalar if q < 3 else nc.sync
+            queue = nc.scalar if q < 2 else nc.sync
             queue.dma_start(out=out_2[0, 4 * q : 4 * q + 4, :].bitcast(I32), in_=o_s[32 * q : 32 * q + 4, :].bitcast(I32))

@@ -69,7 +69,8 @@ def tile_picked_layghardmix_none_po_kernel(
         w2_s = keep.tile([P, N], U8, name="w2_s")
         gain = keep.tile([P, PACK], F32, name="gain")
 
-        nc.vector.memset(x_s[:].bitcast(I32), 0)
+        nc.gpsimd.memset(x_s[:, : T // 2].bitcast(I32), 0)
+        nc.vector.memset(x_s[:, T // 2 :].bitcast(I32), 0)
 
         nc.sync.dma_start(offs_sb[:], offs)
         nc.sync.dma_start(out=w1_w[:], in_=words_of(w1_words))
@@ -107,22 +108,29 @@ def tile_picked_layghardmix_none_po_kernel(
         deal_scales(nc, w1_sd[:], w1_s[:], 0, 1)
         deal_scales(nc, w1_sd[:], w1_s[:], 1, PACK)
 
-        y_ps = [psum.tile([P, S], F32, name=f"y_ps{t}") for t in range(PACK)]
-        h_ps = [psum.tile([P, S], F32, name=f"h_ps{t}") for t in range(PACK)]
-        for t in range(PACK):
-            cols = slice(t * P, (t + 1) * P)
+        def first_product(out, t, columns):
             nc.tensor.matmul_mx(
-                out=y_ps[t][:],
-                lhsT=w1_wd[:, cols].bitcast(FP8X4),
-                lhsT_scale=w1_sd[:, cols],
-                rhs=xg_w[:].bitcast(FP8X4),
-                rhs_scale=xg_s[:],
+                out=out,
+                lhsT=w1_wd[:, t * P : (t + 1) * P].bitcast(FP8X4),
+                lhsT_scale=w1_sd[:, t * P : (t + 1) * P],
+                rhs=xg_w[:, columns].bitcast(FP8X4),
+                rhs_scale=xg_s[:, columns],
                 start=True,
                 stop=True,
             )
-        nc.scalar.copy(out=y_win[0][:, :S], in_=y_ps[0][:])
+
+        y_left = psum.tile([P, HALF], F32, name="y_left", tag="half0")
+        y_right = psum.tile([P, HALF], F32, name="y_right", tag="half1")
+        first_product(y_left[:], 0, slice(0, HALF))
+        first_product(y_right[:], 0, slice(HALF, S))
+        nc.vector.tensor_copy(out=y_win[0][:, :HALF], in_=y_left[:])
+        nc.scalar.copy(out=y_win[0][:, HALF:S], in_=y_right[:])
+        w2_wd = keep.tile([P, N], U32, name="w2_wd", tag="w1 scales, dealt w2 words", align_bytes=64)
+        deal_words(nc, w2_wd[:], w2_w[:].bitcast(U32))
         for t in range(1, PACK):
-            nc.vector.tensor_copy(out=y_win[t][:, :S], in_=y_ps[t][:])
+            y_ps = psum.tile([P, S], F32, name=f"y_ps{t}")
+            first_product(y_ps[:], t, slice(0, S))
+            nc.vector.tensor_copy(out=y_win[t][:, :S], in_=y_ps[:])
 
         z_planes = keep.tile([P, 2, PACK, HALF], BF16, name="z_planes")
         lows = keep.tile([P, PACK, S], F32, name="lows")
@@ -171,46 +179,51 @@ def tile_picked_layghardmix_none_po_kernel(
                 ALU.mult,
             )
 
-        w2_wd = keep.tile([P, N], U32, name="w2_wd", tag="w1 scales, dealt w2 words", align_bytes=64)
-        deal_words(nc, w2_wd[:], w2_w[:].bitcast(U32))
+        w2_sd = keep.tile([P, N], U8, name="w2_sd", tag="w2 words, dealt w2 scales", align_bytes=64)
+        deal_scales(nc, w2_sd[:], w2_s[:], 0, PACK)
         fetch(pieces[0])
-        for i, piece in enumerate(pieces):
-            if i + 1 < len(pieces):
-                fetch(pieces[i + 1])
+        for i, piece in enumerate(pieces[:-1]):
+            fetch(pieces[i + 1])
+            low(piece)
             high(piece)
             gate(piece)
-            low(piece)
-            if i == 0:
-                w2_sd = keep.tile([P, N], U8, name="w2_sd", tag="w2 words, dealt w2 scales", align_bytes=64)
-                deal_scales(nc, w2_sd[:], w2_s[:], 0, PACK)
-            else:
-                mix(pieces[i - 1])
             span(piece)
+            if i > 0:
+                mix(pieces[i - 1])
+        high(pieces[-1])
+        gate(pieces[-1])
+        low(pieces[-1])
+        mix(pieces[-2])
+        span(pieces[-1])
         mix(pieces[-1])
 
         z_w = keep.tile([P, S], U32, name="z_w", align_bytes=64)
         z_s = keep.tile([P, S], U8, name="z_s", align_bytes=64)
         nc.scalar.copy(out=z_rows[0][:], in_=z_planes[:, 0].rearrange("p t j -> p j t"))
         nc.vector.tensor_copy(out=z_rows[1][:], in_=z_planes[:, 1].rearrange("p t j -> p j t"))
+        def second_product(out, t, columns):
+            nc.tensor.matmul_mx(
+                out=out,
+                lhsT=w2_wd[:, t * P : (t + 1) * P].bitcast(FP8X4),
+                lhsT_scale=w2_sd[:, t * P : (t + 1) * P],
+                rhs=z_w[:, columns].bitcast(FP8X4),
+                rhs_scale=z_s[:, columns],
+                start=True,
+                stop=True,
+            )
+
         for u in range(2):
             half = slice(u * HALF, (u + 1) * HALF)
             nc.vector.quantize_mx(
                 out=z_w[:, half].bitcast(FP8X4), scales=z_s[:, half], in_=z_rows[u][:].rearrange("p j t -> p (j t)")
             )
-            for t in range(PACK):
-                cols = slice(t * P, (t + 1) * P)
-                nc.tensor.matmul_mx(
-                    out=h_ps[t][:, half],
-                    lhsT=w2_wd[:, cols].bitcast(FP8X4),
-                    lhsT_scale=w2_sd[:, cols],
-                    rhs=z_w[:, half].bitcast(FP8X4),
-                    rhs_scale=z_s[:, half],
-                    start=True,
-                    stop=True,
-                )
-            nc.scalar.copy(out=h_win[0][:, half], in_=h_ps[0][:, half])
+            h_half = psum.tile([P, HALF], F32, name=f"h_half{u}", tag=f"half{u}")
+            second_product(h_half[:], 0, half)
+            nc.scalar.copy(out=h_win[0][:, half], in_=h_half[:])
         for t in range(1, PACK):
-            nc.vector.tensor_copy(out=h_win[t][:, :S], in_=h_ps[t][:])
+            h_ps = psum.tile([P, S], F32, name=f"h_ps{t}")
+            second_product(h_ps[:], t, slice(0, S))
+            nc.vector.tensor_copy(out=h_win[t][:, :S], in_=h_ps[:])
 
         result = keep.tile([P, 2, PACK, HALF], F32, name="result")
         o_rows = [keep.tile([P, HALF, PACK], BF16, name=f"o_rows{u}", align_bytes=64) for u in range(2)]

@@ -17,18 +17,31 @@ ACT = mybir.ActivationFunctionType
 
 P = 128
 PACK = 4
+QUADRANTS = 4
+QUADRANT = P // QUADRANTS
+SCALE_ROWS = 4
+GROUP = 16
+MEMBERS = J // S
 HALF = S // 2
-Y_WINDOW = J + 16
+
+Y_WINDOW = J + GROUP
 H_WINDOW = 2 * S
 
-
-def load_scale_rows(queue, tile, scales, q):
-    queue.dma_start(out=tile[32 * q : 32 * q + 4, :].bitcast(I32), in_=scales[0, 4 * q : 4 * q + 4, :].bitcast(I32))
+PIECES = [(t, 0, S) for t in range(PACK - 1)] + [(PACK - 1, 0, HALF), (PACK - 1, HALF, S)]
 
 
-def load_scale_rows_spread(queue, tile, scales, q):
+def scale_rows(scales, q):
+    return scales[0, SCALE_ROWS * q : SCALE_ROWS * (q + 1), :].bitcast(I32)
+
+
+def live_partitions(tile, q):
+    return tile[QUADRANT * q : QUADRANT * q + SCALE_ROWS, :].bitcast(I32)
+
+
+def load_scale_rows_repeated(queue, tile, scales, q):
     queue.dma_start(
-        out=tile[32 * q : 32 * q + 32, :].bitcast(I32), in_=scales[0, 4 * q : 4 * q + 4, :].bitcast(I32).partition_broadcast(8)
+        out=tile[QUADRANT * q : QUADRANT * (q + 1), :].bitcast(I32),
+        in_=scale_rows(scales, q).partition_broadcast(QUADRANT // SCALE_ROWS),
     )
 
 
@@ -46,6 +59,23 @@ def deal_words(nc, dealt, raw):
     nc.vector.tensor_copy(out=dealt.rearrange("p (t m) -> p m t", t=PACK), in_=raw.rearrange("p (m t) -> p m t", t=PACK))
 
 
+def product(nc, out, weight_words, weight_scales, t, words, scales, columns):
+    plane = slice(t * P, (t + 1) * P)
+    nc.tensor.matmul_mx(
+        out=out,
+        lhsT=weight_words[:, plane].bitcast(FP8X4),
+        lhsT_scale=weight_scales[:, plane],
+        rhs=words[:, columns].bitcast(FP8X4),
+        rhs_scale=scales[:, columns],
+        start=True,
+        stop=True,
+    )
+
+
+def by_halves(columns):
+    return columns.rearrange("p (u j) -> p u j", j=HALF)
+
+
 def tile_picked_layghardmix_none_po_kernel(
     tc, x_words, x_scales, w1_words, w1_scales, gn, w2_words, w2_scales, offs, n1, n2, n3, n4, out_0, out_1, out_2
 ):
@@ -55,13 +85,13 @@ def tile_picked_layghardmix_none_po_kernel(
         ring = ctx.enter_context(tc.tile_pool(name="ring", bufs=2))
         psum = ctx.enter_context(tc.psum_pool(name="psum", bufs=1))
 
-        offs_sb = keep.tile([P, S // 16], U16, name="offs_sb")
-        n1_sb = keep.tile([P, J // 16], U16, name="n1_sb")
-        n2_sb = keep.tile([P, S // 16], U16, name="n2_sb")
-        n3_sb = keep.tile([P, S // 16], U16, name="n3_sb")
-        n4_sb = keep.tile([P, S // 16], U16, name="n4_sb")
+        offs_sb = keep.tile([P, S // GROUP], U16, name="offs_sb")
+        n1_sb = keep.tile([P, J // GROUP], U16, name="n1_sb")
+        n2_sb = keep.tile([P, S // GROUP], U16, name="n2_sb")
+        n3_sb = keep.tile([P, S // GROUP], U16, name="n3_sb")
+        n4_sb = keep.tile([P, S // GROUP], U16, name="n4_sb")
 
-        x_w = keep.tile([P, T], I32, name="x_w", tag="x words, dealt w1 scales", align_bytes=64)
+        x_w = keep.tile([P, T], I32, name="x_w")
         x_s = keep.tile([P, T], U8, name="x_s", tag="x scales, picked words", align_bytes=64)
         w1_w = keep.tile([P, H], I32, name="w1_w")
         w1_s = keep.tile([P, H], U8, name="w1_s", tag="w1 scales, dealt w2 words", align_bytes=64)
@@ -74,16 +104,17 @@ def tile_picked_layghardmix_none_po_kernel(
 
         nc.sync.dma_start(offs_sb[:], offs)
         nc.sync.dma_start(out=w1_w[:], in_=words_of(w1_words))
-        load_scale_rows_spread(nc.scalar, w1_s, w1_scales, 0)
-        for q in range(4):
-            load_scale_rows(nc.sync if q < 2 else nc.scalar, x_s, x_scales, q)
+        load_scale_rows_repeated(nc.scalar, w1_s, w1_scales, 0)
+        for q in range(QUADRANTS):
+            queue = nc.sync if q < QUADRANTS // 2 else nc.scalar
+            queue.dma_start(out=live_partitions(x_s, q), in_=scale_rows(x_scales, q))
         nc.sync.dma_start(out=x_w[:], in_=words_of(x_words))
-        for q in range(1, 4):
-            load_scale_rows_spread(nc.sync, w1_s, w1_scales, q)
+        for q in range(1, QUADRANTS):
+            load_scale_rows_repeated(nc.sync, w1_s, w1_scales, q)
         nc.sync.dma_start(n1_sb[:], n1)
         nc.sync.dma_start(out=w2_w[:], in_=words_of(w2_words))
-        for q in range(4):
-            load_scale_rows_spread(nc.sync, w2_s, w2_scales, q)
+        for q in range(QUADRANTS):
+            load_scale_rows_repeated(nc.sync, w2_s, w2_scales, q)
         nc.sync.dma_start(out=gain[:], in_=gn.rearrange("(p t) o -> p (t o)", t=PACK))
         nc.sync.dma_start(n3_sb[:], n3)
         nc.sync.dma_start(n4_sb[:], n4)
@@ -104,32 +135,21 @@ def tile_picked_layghardmix_none_po_kernel(
         nc.vector.tensor_copy(out=xg_s[:], in_=x_s[:].indirect(offs_sb[:]))
         xg_w = keep.tile([P, S], U32, name="xg_w", tag="x scales, picked words", align_bytes=64)
         nc.vector.tensor_copy(out=xg_w[:], in_=x_w[:].bitcast(U32).indirect(offs_sb[:]))
-        w1_sd = keep.tile([P, H], U8, name="w1_sd", tag="x words, dealt w1 scales", align_bytes=64)
+        w1_sd = keep.tile([P, H], U8, name="w1_sd", align_bytes=64)
         deal_scales(nc, w1_sd[:], w1_s[:], 0, 1)
         deal_scales(nc, w1_sd[:], w1_s[:], 1, PACK)
 
-        def first_product(out, t, columns):
-            nc.tensor.matmul_mx(
-                out=out,
-                lhsT=w1_wd[:, t * P : (t + 1) * P].bitcast(FP8X4),
-                lhsT_scale=w1_sd[:, t * P : (t + 1) * P],
-                rhs=xg_w[:, columns].bitcast(FP8X4),
-                rhs_scale=xg_s[:, columns],
-                start=True,
-                stop=True,
-            )
-
         y_left = psum.tile([P, HALF], F32, name="y_left", tag="half0")
         y_right = psum.tile([P, HALF], F32, name="y_right", tag="half1")
-        first_product(y_left[:], 0, slice(0, HALF))
-        first_product(y_right[:], 0, slice(HALF, S))
+        product(nc, y_left[:], w1_wd, w1_sd, 0, xg_w, xg_s, slice(0, HALF))
+        product(nc, y_right[:], w1_wd, w1_sd, 0, xg_w, xg_s, slice(HALF, S))
         nc.vector.tensor_copy(out=y_win[0][:, :HALF], in_=y_left[:])
         nc.scalar.copy(out=y_win[0][:, HALF:S], in_=y_right[:])
         w2_wd = keep.tile([P, N], U32, name="w2_wd", tag="w1 scales, dealt w2 words", align_bytes=64)
         deal_words(nc, w2_wd[:], w2_w[:].bitcast(U32))
         for t in range(1, PACK):
             y_ps = psum.tile([P, S], F32, name=f"y_ps{t}")
-            first_product(y_ps[:], t, slice(0, S))
+            product(nc, y_ps[:], w1_wd, w1_sd, t, xg_w, xg_s, slice(0, S))
             nc.vector.tensor_copy(out=y_win[t][:, :S], in_=y_ps[:])
 
         z_planes = keep.tile([P, 2, PACK, HALF], BF16, name="z_planes")
@@ -137,28 +157,28 @@ def tile_picked_layghardmix_none_po_kernel(
         highs = keep.tile([P, PACK, S], F32, name="highs")
         gates = keep.tile([P, PACK, S], F32, name="gates")
         spans = keep.tile([P, PACK, S], F32, name="spans")
-        pieces = [(0, 0, S), (1, 0, S), (2, 0, S), (3, 0, HALF), (3, HALF, S)]
         members = {}
         z_rows = [keep.tile([P, HALF, PACK], BF16, name=f"z_rows{u}", align_bytes=64) for u in range(2)]
 
         def fetch(piece):
             t, j0, j1 = piece
-            members[piece] = ring.tile([P, 2 * (j1 - j0)], F32, name="members")
-            nc.scalar.activation(members[piece][:], y_win[t][:].indirect(n1_sb[:, j0 // 8 : j1 // 8]), ACT.Copy)
+            members[piece] = ring.tile([P, MEMBERS * (j1 - j0)], F32, name="members")
+            entries = slice(MEMBERS * j0 // GROUP, MEMBERS * j1 // GROUP)
+            nc.scalar.activation(members[piece][:], y_win[t][:].indirect(n1_sb[:, entries]), ACT.Copy)
 
         def pair(piece):
-            both = members[piece][:].rearrange("p (j e) -> p j e", e=2)
+            both = members[piece][:].rearrange("p (j e) -> p j e", e=MEMBERS)
             return both[:, :, 0], both[:, :, 1]
 
         def high(piece):
             t, j0, j1 = piece
-            a, b = pair(piece)
-            nc.vector.tensor_tensor(highs[:, t, j0:j1], a, b, ALU.max)
+            first, second = pair(piece)
+            nc.vector.tensor_tensor(highs[:, t, j0:j1], first, second, ALU.max)
 
         def low(piece):
             t, j0, j1 = piece
-            a, b = pair(piece)
-            nc.vector.tensor_tensor(lows[:, t, j0:j1], a, b, ALU.min)
+            first, second = pair(piece)
+            nc.vector.tensor_tensor(lows[:, t, j0:j1], first, second, ALU.min)
 
         def gate(piece):
             t, j0, j1 = piece
@@ -172,86 +192,71 @@ def tile_picked_layghardmix_none_po_kernel(
             t, j0, j1 = piece
             nc.vector.scalar_tensor_tensor(
                 z_planes[:, j0 // HALF : j1 // HALF, t, :],
-                spans[:, t, j0:j1].rearrange("p (u j) -> p u j", j=HALF),
+                by_halves(spans[:, t, j0:j1]),
                 gain[:, t : t + 1],
-                gates[:, t, j0:j1].rearrange("p (u j) -> p u j", j=HALF),
+                by_halves(gates[:, t, j0:j1]),
                 ALU.mult,
                 ALU.mult,
             )
 
         w2_sd = keep.tile([P, N], U8, name="w2_sd", tag="w2 words, dealt w2 scales", align_bytes=64)
         deal_scales(nc, w2_sd[:], w2_s[:], 0, PACK)
-        fetch(pieces[0])
-        for i, piece in enumerate(pieces[:-1]):
-            fetch(pieces[i + 1])
+        fetch(PIECES[0])
+        for i, piece in enumerate(PIECES[:-1]):
+            fetch(PIECES[i + 1])
             low(piece)
             high(piece)
             gate(piece)
             span(piece)
             if i > 0:
-                mix(pieces[i - 1])
-        high(pieces[-1])
-        gate(pieces[-1])
-        low(pieces[-1])
-        mix(pieces[-2])
-        span(pieces[-1])
-        mix(pieces[-1])
+                mix(PIECES[i - 1])
+        high(PIECES[-1])
+        gate(PIECES[-1])
+        low(PIECES[-1])
+        mix(PIECES[-2])
+        span(PIECES[-1])
+        mix(PIECES[-1])
 
         z_w = keep.tile([P, S], U32, name="z_w", align_bytes=64)
         z_s = keep.tile([P, S], U8, name="z_s", align_bytes=64)
         nc.scalar.copy(out=z_rows[0][:], in_=z_planes[:, 0].rearrange("p t j -> p j t"))
         nc.vector.tensor_copy(out=z_rows[1][:], in_=z_planes[:, 1].rearrange("p t j -> p j t"))
-        def second_product(out, t, columns):
-            nc.tensor.matmul_mx(
-                out=out,
-                lhsT=w2_wd[:, t * P : (t + 1) * P].bitcast(FP8X4),
-                lhsT_scale=w2_sd[:, t * P : (t + 1) * P],
-                rhs=z_w[:, columns].bitcast(FP8X4),
-                rhs_scale=z_s[:, columns],
-                start=True,
-                stop=True,
-            )
-
         for u in range(2):
             half = slice(u * HALF, (u + 1) * HALF)
             nc.vector.quantize_mx(
                 out=z_w[:, half].bitcast(FP8X4), scales=z_s[:, half], in_=z_rows[u][:].rearrange("p j t -> p (j t)")
             )
             h_half = psum.tile([P, HALF], F32, name=f"h_half{u}", tag=f"half{u}")
-            second_product(h_half[:], 0, half)
+            product(nc, h_half[:], w2_wd, w2_sd, 0, z_w, z_s, half)
             nc.scalar.copy(out=h_win[0][:, half], in_=h_half[:])
         for t in range(1, PACK):
             h_ps = psum.tile([P, S], F32, name=f"h_ps{t}")
-            second_product(h_ps[:], t, slice(0, S))
+            product(nc, h_ps[:], w2_wd, w2_sd, t, z_w, z_s, slice(0, S))
             nc.vector.tensor_copy(out=h_win[t][:, :S], in_=h_ps[:])
 
         result = keep.tile([P, 2, PACK, HALF], F32, name="result")
         o_rows = [keep.tile([P, HALF, PACK], BF16, name=f"o_rows{u}", align_bytes=64) for u in range(2)]
         o_w = keep.tile([P, S], I32, name="o_w", align_bytes=64)
         o_s = keep.tile([P, S], U8, name="o_s", align_bytes=64)
-        out_rows = out_0.rearrange("(p t) (u j) -> p u t j", t=PACK, j=HALF)
+        out_planes = out_0.rearrange("(p t) (u j) -> p u t j", t=PACK, j=HALF)
         out_words = words_of(out_1)
 
-        for t, j0, j1 in pieces:
+        for t, j0, j1 in PIECES:
             at3 = ring.tile([P, j1 - j0], F32, name="at3")
             at4 = ring.tile([P, j1 - j0], F32, name="at4")
             at2 = ring.tile([P, j1 - j0], F32, name="at2")
-            right = ring.tile([P, j1 - j0], F32, name="right")
-            left = ring.tile([P, j1 - j0], F32, name="left")
-            entries = slice(j0 // 16, j1 // 16)
+            subtrahend = ring.tile([P, j1 - j0], F32, name="subtrahend")
+            minuend = ring.tile([P, j1 - j0], F32, name="minuend")
+            entries = slice(j0 // GROUP, j1 // GROUP)
             halves = slice(j0 // HALF, j1 // HALF)
             nc.scalar.activation(at3[:], h_win[t][:].indirect(n3_sb[:, entries]), ACT.Copy)
             nc.scalar.activation(at4[:], h_win[t][:].indirect(n4_sb[:, entries]), ACT.Copy)
             nc.scalar.activation(at2[:], h_win[t][:].indirect(n2_sb[:, entries]), ACT.Copy)
-            nc.vector.tensor_tensor(right[:], at3[:], at4[:], ALU.max)
-            nc.vector.tensor_tensor(left[:], h_win[t][:, j0:j1], at2[:], ALU.max)
-            nc.vector.tensor_tensor(
-                result[:, halves, t, :],
-                left[:].rearrange("p (u j) -> p u j", j=HALF),
-                right[:].rearrange("p (u j) -> p u j", j=HALF),
-                ALU.subtract,
-            )
-            nc.sync.dma_start(out=out_rows[:, halves, t, :], in_=result[:, halves, t, :])
+            nc.vector.tensor_tensor(subtrahend[:], at3[:], at4[:], ALU.max)
+            nc.vector.tensor_tensor(minuend[:], h_win[t][:, j0:j1], at2[:], ALU.max)
+            nc.vector.tensor_tensor(result[:, halves, t, :], by_halves(minuend[:]), by_halves(subtrahend[:]), ALU.subtract)
+            nc.sync.dma_start(out=out_planes[:, halves, t, :], in_=result[:, halves, t, :])
+
         nc.scalar.copy(out=o_rows[0][:], in_=result[:, 0].rearrange("p t j -> p j t"))
         nc.vector.tensor_copy(out=o_rows[1][:], in_=result[:, 1].rearrange("p t j -> p j t"))
         for u in range(2):
@@ -260,6 +265,6 @@ def tile_picked_layghardmix_none_po_kernel(
                 out=o_w[:, half].bitcast(FP8X4), scales=o_s[:, half], in_=o_rows[u][:].rearrange("p j t -> p (j t)")
             )
             nc.sync.dma_start(out=out_words[:, half], in_=o_w[:, half])
-        for q in range(4):
-            queue = nc.scalar if q < 2 else nc.sync
-            queue.dma_start(out=out_2[0, 4 * q : 4 * q + 4, :].bitcast(I32), in_=o_s[32 * q : 32 * q + 4, :].bitcast(I32))
+        for q in range(QUADRANTS):
+            queue = nc.scalar if q < QUADRANTS // 2 else nc.sync
+            queue.dma_start(out=scale_rows(out_2, q), in_=live_partitions(o_s, q))

from contextlib import ExitStack

import concourse.mybir as mybir

K, T, S, N, H, J = 512, 2048, 256, 512, 512, 512
FLOPS = 2 * K * H * S + 2 * H * N * S

F32 = mybir.dt.float32
BF16 = mybir.dt.bfloat16
I32 = mybir.dt.int32
U32 = mybir.dt.uint32
U16 = mybir.dt.uint16
U8 = mybir.dt.uint8
FP8X4 = mybir.dt.float8_e4m3fn_x4
ALU = mybir.AluOpType
ACT = mybir.ActivationFunctionType

P = 128
PACK = 4
QUADRANTS = 4
QUADRANT = P // QUADRANTS
SCALE_ROWS = 4
GROUP = 16
MEMBERS = J // S
HALF = S // 2

Y_WINDOW = J + GROUP
H_WINDOW = 2 * S

PIECES = [(t, 0, S) for t in range(PACK - 1)] + [(PACK - 1, 0, HALF), (PACK - 1, HALF, S)]


def scale_rows(scales, q):
    return scales[0, SCALE_ROWS * q : SCALE_ROWS * (q + 1), :].bitcast(I32)


def live_partitions(tile, q):
    return tile[QUADRANT * q : QUADRANT * q + SCALE_ROWS, :].bitcast(I32)


def load_scale_rows_repeated(queue, tile, scales, q):
    queue.dma_start(
        out=tile[QUADRANT * q : QUADRANT * (q + 1), :].bitcast(I32),
        in_=scale_rows(scales, q).partition_broadcast(QUADRANT // SCALE_ROWS),
    )


def words_of(packed):
    return packed[0].rearrange("p n t -> p (n t)").bitcast(I32)


def deal_scales(nc, dealt, raw, t0, t1):
    nc.vector.tensor_copy(
        out=dealt.rearrange("p (t m) -> p t m", t=PACK)[:, t0:t1, :], in_=raw.rearrange("p (m t) -> p t m", t=PACK)[:, t0:t1, :]
    )


def deal_words(nc, dealt, raw):
    nc.vector.tensor_copy(out=dealt.rearrange("p (t m) -> p m t", t=PACK), in_=raw.rearrange("p (m t) -> p m t", t=PACK))


def product(nc, out, weight_words, weight_scales, t, words, scales, columns):
    plane = slice(t * P, (t + 1) * P)
    nc.tensor.matmul_mx(
        out=out,
        lhsT=weight_words[:, plane].bitcast(FP8X4),
        lhsT_scale=weight_scales[:, plane],
        rhs=words[:, columns].bitcast(FP8X4),
        rhs_scale=scales[:, columns],
        start=True,
        stop=True,
    )


def by_halves(columns):
    return columns.rearrange("p (u j) -> p u j", j=HALF)


def tile_picked_layghardmix_none_po_kernel(
    tc, x_words, x_scales, w1_words, w1_scales, gn, w2_words, w2_scales, offs, n1, n2, n3, n4, out_0, out_1, out_2
):
    nc = tc.nc
    with ExitStack() as ctx:
        keep = ctx.enter_context(tc.tile_pool(name="keep", bufs=1))
        ring = ctx.enter_context(tc.tile_pool(name="ring", bufs=2))
        psum = ctx.enter_context(tc.psum_pool(name="psum", bufs=1))

        offs_sb = keep.tile([P, S // GROUP], U16, name="offs_sb")
        n1_sb = keep.tile([P, J // GROUP], U16, name="n1_sb")
        n2_sb = keep.tile([P, S // GROUP], U16, name="n2_sb")
        n3_sb = keep.tile([P, S // GROUP], U16, name="n3_sb")
        n4_sb = keep.tile([P, S // GROUP], U16, name="n4_sb")

        x_w = keep.tile([P, T], I32, name="x_w")
        x_s = keep.tile([P, T], U8, name="x_s", tag="x scales, picked words", align_bytes=64)
        w1_w = keep.tile([P, H], I32, name="w1_w")
        w1_s = keep.tile([P, H], U8, name="w1_s", tag="w1 scales, dealt w2 words", align_bytes=64)
        w2_w = keep.tile([P, N], I32, name="w2_w", tag="w2 words, dealt w2 scales", align_bytes=64)
        w2_s = keep.tile([P, N], U8, name="w2_s")
        gain = keep.tile([P, PACK], F32, name="gain")

        nc.gpsimd.memset(x_s[:, : T // 2].bitcast(I32), 0)
        nc.vector.memset(x_s[:, T // 2 :].bitcast(I32), 0)

        nc.sync.dma_start(offs_sb[:], offs)
        nc.sync.dma_start(out=w1_w[:], in_=words_of(w1_words))
        load_scale_rows_repeated(nc.scalar, w1_s, w1_scales, 0)
        for q in range(QUADRANTS):
            queue = nc.sync if q < QUADRANTS // 2 else nc.scalar
            queue.dma_start(out=live_partitions(x_s, q), in_=scale_rows(x_scales, q))
        nc.sync.dma_start(out=x_w[:], in_=words_of(x_words))
        for q in range(1, QUADRANTS):
            load_scale_rows_repeated(nc.sync, w1_s, w1_scales, q)
        nc.sync.dma_start(n1_sb[:], n1)
        nc.sync.dma_start(out=w2_w[:], in_=words_of(w2_words))
        for q in range(QUADRANTS):
            load_scale_rows_repeated(nc.sync, w2_s, w2_scales, q)
        nc.sync.dma_start(out=gain[:], in_=gn.rearrange("(p t) o -> p (t o)", t=PACK))
        nc.sync.dma_start(n3_sb[:], n3)
        nc.sync.dma_start(n4_sb[:], n4)
        nc.sync.dma_start(n2_sb[:], n2)

        y_win = [keep.tile([P, Y_WINDOW], F32, name=f"y_win{t}") for t in range(PACK)]
        h_win = [keep.tile([P, H_WINDOW], F32, name=f"h_win{t}") for t in range(PACK)]
        for t in range(PACK):
            nc.vector.memset(y_win[t][:, S:], 0.0)
        for t in range(PACK):
            nc.vector.memset(h_win[t][:, S:], 0.0)
        warm = keep.tile([P, 1], F32, name="warm")
        nc.scalar.activation(warm[:], y_win[0][:, S : S + 1], ACT.Sigmoid)

        w1_wd = keep.tile([P, H], U32, name="w1_wd", align_bytes=64)
        deal_words(nc, w1_wd[:], w1_w[:].bitcast(U32))
        xg_s = keep.tile([P, S], U8, name="xg_s", align_bytes=64)
        nc.vector.tensor_copy(out=xg_s[:], in_=x_s[:].indirect(offs_sb[:]))
        xg_w = keep.tile([P, S], U32, name="xg_w", tag="x scales, picked words", align_bytes=64)
        nc.vector.tensor_copy(out=xg_w[:], in_=x_w[:].bitcast(U32).indirect(offs_sb[:]))
        w1_sd = keep.tile([P, H], U8, name="w1_sd", align_bytes=64)
        deal_scales(nc, w1_sd[:], w1_s[:], 0, 1)
        deal_scales(nc, w1_sd[:], w1_s[:], 1, PACK)

        y_left = psum.tile([P, HALF], F32, name="y_left", tag="half0")
        y_right = psum.tile([P, HALF], F32, name="y_right", tag="half1")
        product(nc, y_left[:], w1_wd, w1_sd, 0, xg_w, xg_s, slice(0, HALF))
        product(nc, y_right[:], w1_wd, w1_sd, 0, xg_w, xg_s, slice(HALF, S))
        nc.vector.tensor_copy(out=y_win[0][:, :HALF], in_=y_left[:])
        nc.scalar.copy(out=y_win[0][:, HALF:S], in_=y_right[:])
        w2_wd = keep.tile([P, N], U32, name="w2_wd", tag="w1 scales, dealt w2 words", align_bytes=64)
        deal_words(nc, w2_wd[:], w2_w[:].bitcast(U32))
        for t in range(1, PACK):
            y_ps = psum.tile([P, S], F32, name=f"y_ps{t}")
            product(nc, y_ps[:], w1_wd, w1_sd, t, xg_w, xg_s, slice(0, S))
            nc.vector.tensor_copy(out=y_win[t][:, :S], in_=y_ps[:])

        z_planes = keep.tile([P, 2, PACK, HALF], BF16, name="z_planes")
        lows = keep.tile([P, PACK, S], F32, name="lows")
        highs = keep.tile([P, PACK, S], F32, name="highs")
        gates = keep.tile([P, PACK, S], F32, name="gates")
        spans = keep.tile([P, PACK, S], F32, name="spans")
        members = {}
        z_rows = [keep.tile([P, HALF, PACK], BF16, name=f"z_rows{u}", align_bytes=64) for u in range(2)]

        def fetch(piece):
            t, j0, j1 = piece
            members[piece] = ring.tile([P, MEMBERS * (j1 - j0)], F32, name="members")
            entries = slice(MEMBERS * j0 // GROUP, MEMBERS * j1 // GROUP)
            nc.scalar.activation(members[piece][:], y_win[t][:].indirect(n1_sb[:, entries]), ACT.Copy)

        def pair(piece):
            both = members[piece][:].rearrange("p (j e) -> p j e", e=MEMBERS)
            return both[:, :, 0], both[:, :, 1]

        def high(piece):
            t, j0, j1 = piece
            first, second = pair(piece)
            nc.vector.tensor_tensor(highs[:, t, j0:j1], first, second, ALU.max)

        def low(piece):
            t, j0, j1 = piece
            first, second = pair(piece)
            nc.vector.tensor_tensor(lows[:, t, j0:j1], first, second, ALU.min)

        def gate(piece):
            t, j0, j1 = piece
            nc.scalar.activation(gates[:, t, j0:j1], highs[:, t, j0:j1], ACT.Sigmoid)

        def span(piece):
            t, j0, j1 = piece
            nc.vector.tensor_tensor(spans[:, t, j0:j1], y_win[t][:, j0:j1], lows[:, t, j0:j1], ALU.subtract)

        def mix(piece):
            t, j0, j1 = piece
            nc.vector.scalar_tensor_tensor(
                z_planes[:, j0 // HALF : j1 // HALF, t, :],
                by_halves(spans[:, t, j0:j1]),
                gain[:, t : t + 1],
                by_halves(gates[:, t, j0:j1]),
                ALU.mult,
                ALU.mult,
            )

        w2_sd = keep.tile([P, N], U8, name="w2_sd", tag="w2 words, dealt w2 scales", align_bytes=64)
        deal_scales(nc, w2_sd[:], w2_s[:], 0, PACK)
        fetch(PIECES[0])
        for i, piece in enumerate(PIECES[:-1]):
            fetch(PIECES[i + 1])
            low(piece)
            high(piece)
            gate(piece)
            span(piece)
            if i > 0:
                mix(PIECES[i - 1])
        high(PIECES[-1])
        gate(PIECES[-1])
        low(PIECES[-1])
        mix(PIECES[-2])
        span(PIECES[-1])
        mix(PIECES[-1])

        z_w = keep.tile([P, S], U32, name="z_w", align_bytes=64)
        z_s = keep.tile([P, S], U8, name="z_s", align_bytes=64)
        nc.scalar.copy(out=z_rows[0][:], in_=z_planes[:, 0].rearrange("p t j -> p j t"))
        nc.vector.tensor_copy(out=z_rows[1][:], in_=z_planes[:, 1].rearrange("p t j -> p j t"))
        for u in range(2):
            half = slice(u * HALF, (u + 1) * HALF)
            nc.vector.quantize_mx(
                out=z_w[:, half].bitcast(FP8X4), scales=z_s[:, half], in_=z_rows[u][:].rearrange("p j t -> p (j t)")
            )
            h_half = psum.tile([P, HALF], F32, name=f"h_half{u}", tag=f"half{u}")
            product(nc, h_half[:], w2_wd, w2_sd, 0, z_w, z_s, half)
            nc.scalar.copy(out=h_win[0][:, half], in_=h_half[:])
        for t in range(1, PACK):
            h_ps = psum.tile([P, S], F32, name=f"h_ps{t}")
            product(nc, h_ps[:], w2_wd, w2_sd, t, z_w, z_s, slice(0, S))
            nc.vector.tensor_copy(out=h_win[t][:, :S], in_=h_ps[:])

        result = keep.tile([P, 2, PACK, HALF], F32, name="result")
        o_rows = [keep.tile([P, HALF, PACK], BF16, name=f"o_rows{u}", align_bytes=64) for u in range(2)]
        o_w = keep.tile([P, S], I32, name="o_w", align_bytes=64)
        o_s = keep.tile([P, S], U8, name="o_s", align_bytes=64)
        out_planes = out_0.rearrange("(p t) (u j) -> p u t j", t=PACK, j=HALF)
        out_words = words_of(out_1)

        for t, j0, j1 in PIECES:
            at3 = ring.tile([P, j1 - j0], F32, name="at3")
            at4 = ring.tile([P, j1 - j0], F32, name="at4")
            at2 = ring.tile([P, j1 - j0], F32, name="at2")
            subtrahend = ring.tile([P, j1 - j0], F32, name="subtrahend")
            minuend = ring.tile([P, j1 - j0], F32, name="minuend")
            entries = slice(j0 // GROUP, j1 // GROUP)
            halves = slice(j0 // HALF, j1 // HALF)
            nc.scalar.activation(at3[:], h_win[t][:].indirect(n3_sb[:, entries]), ACT.Copy)
            nc.scalar.activation(at4[:], h_win[t][:].indirect(n4_sb[:, entries]), ACT.Copy)
            nc.scalar.activation(at2[:], h_win[t][:].indirect(n2_sb[:, entries]), ACT.Copy)
            nc.vector.tensor_tensor(subtrahend[:], at3[:], at4[:], ALU.max)
            nc.vector.tensor_tensor(minuend[:], h_win[t][:, j0:j1], at2[:], ALU.max)
            nc.vector.tensor_tensor(result[:, halves, t, :], by_halves(minuend[:]), by_halves(subtrahend[:]), ALU.subtract)
            nc.sync.dma_start(out=out_planes[:, halves, t, :], in_=result[:, halves, t, :])

        nc.scalar.copy(out=o_rows[0][:], in_=result[:, 0].rearrange("p t j -> p j t"))
        nc.vector.tensor_copy(out=o_rows[1][:], in_=result[:, 1].rearrange("p t j -> p j t"))
        for u in range(2):
            half = slice(u * HALF, (u + 1) * HALF)
            nc.vector.quantize_mx(
                out=o_w[:, half].bitcast(FP8X4), scales=o_s[:, half], in_=o_rows[u][:].rearrange("p j t -> p (j t)")
            )
            nc.sync.dma_start(out=out_words[:, half], in_=o_w[:, half])
        for q in range(QUADRANTS):
            queue = nc.scalar if q < QUADRANTS // 2 else nc.sync
            queue.dma_start(out=scale_rows(out_2, q), in_=live_partitions(o_s, q))
